import numpy as np, ml_dtypes
CORES = [10,34,74,98]
N = 4
import mx_ref
BF = ml_dtypes.bfloat16
def entries(a):
    return np.ascontiguousarray(a.T).reshape(-1)
def table(e):
    return np.ascontiguousarray(np.reshape(e, (-1, 16)).T).astype(np.int32)
def cols(t, e):
    v = np.concatenate([t.reshape(128, -1, 4), np.zeros((128, 1, 4), BF)], axis=1)
    return np.ascontiguousarray(v[:, e]).reshape(128, -1)
def tile(rs):
    return np.stack(rs, axis=2).reshape(128, -1).astype(BF)
def cut(t, i, w=512):
    return t[:, w * i:w * i + w]
def rowtile(v, k):
    z = np.concatenate([v, np.zeros((1, v.shape[1]), BF)])
    return np.concatenate([np.ascontiguousarray(z[k[:, 4 * m:4 * m + 4]].transpose(0, 2, 1)).reshape(128, -1) for m in range(k.shape[1] // 4)], axis=1)
def f(rng, *shape):
    return mx_ref.flush((rng.standard_normal(shape, dtype=np.float32) * np.exp2(rng.integers(-2, 3, shape[:-1] + (1,)))).astype(BF))
def wide(rng, *shape, cols=0):
    v = rng.standard_normal(shape, dtype=np.float32) * np.exp2(rng.integers(-12, 13, shape)).astype(np.float32)
    if cols: v *= np.repeat(np.exp2(rng.integers(-cols, cols + 1, shape[:-2] + (1, shape[-1] // 4))) * (rng.random(shape[:-2] + (1, shape[-1] // 4)) > 0.0625), 4, axis=-1).astype(np.float32)
    return mx_ref.flush(v.astype(BF))
T, HU, ACT = 128, 1536, 512
def lists(rng, how=None):
    a = []
    for r in range(N):
        e = rng.permutation(HU)[:ACT]
        if how == "reversed": e = np.sort(e)[::-1]
        if how == "clustered": e = rng.integers(0, HU - ACT + 1) + np.arange(ACT)
        a.append(e)
    return {"act": np.stack([e.reshape(128, 4).astype(np.int32) for e in a]), "actc": np.stack([table(e) for e in a])}
def setup_inputs(rng):
    return {"x": f(rng, N, 128, 4 * T), "w1": f(rng, N, 128, 4 * HU), "w2": f(rng, N, HU, 512), **lists(rng)}
def setup_inputs_clustered(rng):
    return {**setup_inputs(rng), **lists(rng, "clustered")}
def setup_inputs_dead(rng):
    d = setup_inputs(rng); d["x"] = np.abs(d["x"])
    for r in range(N):
        k = d["act"][r].reshape(-1)[rng.permutation(ACT)[:ACT // 2]]
        w = d["w1"][r].reshape(128, HU, 4)
        w[:, k] = -np.abs(w[:, k])
        d["w1"][r] = w.reshape(128, -1)
    return d
def setup_inputs_giant(rng):
    d = setup_inputs(rng)
    for r in range(N):
        k = d["act"][r].reshape(-1)[rng.permutation(ACT)[:ACT // 32]]
        d["w2"][r, k] = (d["w2"][r, k].astype(np.float32) * np.float32(4096)).astype(BF)
    return d
def setup_inputs_reversed(rng):
    return {**setup_inputs(rng), **lists(rng, "reversed")}
def setup_inputs_spread(rng):
    d = setup_inputs(rng); d["x"] = wide(rng, N, 128, 4 * T); d["w2"] = wide(rng, N, HU, 512); return d
def check_inputs(d):
    b = []
    for r in range(N):
        e = d["act"][r].reshape(-1)
        if e.min() < 0 or e.max() >= HU or len(set(e.tolist())) != ACT: b.append("act")
        if (entries(d["actc"][r]) != e).any(): b.append("actc")
    return b
def reference(x, w1, w2, act, actc):
    y = np.zeros((N, 128, 4 * T), np.float32)
    X = [mx_ref.quantize(x[r]) for r in range(N)]
    for s in range(N):
        A = [mx_ref.quantize(cols(w1[s], act[s][:, b])) for b in range(4)]
        rows = rowtile(w2[s], act[s])
        B = [mx_ref.quantize(np.ascontiguousarray(cut(rows, o))) for o in range(4)]
        for r in range(N):
            H = mx_ref.quantize(tile([np.maximum(mx_ref.matmul(A[b], X[r]), np.float32(0)) * np.float32(0.05) for b in range(4)]))
            for o in range(4): y[r][:, T * o:T * o + T] += mx_ref.matmul(B[o], H)
    return {"y": y}

@@ -1,0 +1,214 @@
+from concourse.bass import DstId, RemoteDMATransfer, IndirectOffsetOnAxis
+from concourse.mybir import dt, AluOpType, ActivationFunctionType
+
+T_ = 128
+HU = 1536
+ACT = 512
+F8 = "float8_e4m3fn_x4"
+
+SCRATCH = {
+    "actb": ("sbuf", [128, 4], "int32"),
+    "lst": ("sbuf", [128, 64], "int32"),
+    "lf": ("sbuf", [128, 128], "float32"),
+    "lt": ("sbuf", [128, 128], "float32"),
+    "lc": ("sbuf", [128, 32], "float32"),
+    "off": ("sbuf", [128, 128], "uint16"),
+    "xb": ("sbuf", [128, 4 * T_], "bfloat16"),
+    "w1b": ("sbuf", [128, 4 * HU], "bfloat16"),
+    "ab": ("sbuf", [128, 4 * ACT], "bfloat16"),
+    "w2g": ("sbuf", [128, 4 * 512], "bfloat16"),
+    "bb": ("sbuf", [128, 4 * 512], "bfloat16"),
+    "hb": ("sbuf", [128, 4 * 4 * T_], "bfloat16"),
+    "xq": ("sbuf", [128, 4 * T_], F8), "xs": ("sbuf", [128, 4 * T_], "uint8"),
+    "aq": ("sbuf", [128, ACT], F8), "as_": ("sbuf", [128, ACT], "uint8"),
+    "bq": ("sbuf", [128, 512], F8), "bs": ("sbuf", [128, 512], "uint8"),
+    "hq": ("sbuf", [128, 4 * T_], F8), "hs": ("sbuf", [128, 4 * T_], "uint8"),
+    "hinq": ("sbuf", [128, 4 * T_], F8), "hins": ("sbuf", [128, 4 * T_], "uint8"),
+    "binq": ("sbuf", [128, 4 * 512], F8), "bins": ("sbuf", [128, 4 * 512], "uint8"),
+    "rlq": ("sbuf", [128, 256], F8), "rls": ("sbuf", [128, 256], "uint8"),
+    "ysb": ("sbuf", [128, 4 * T_], "float32"),
+    "zp": ("psum", [128, 2048], "float32"),
+    "yp": ("psum", [128, 2048], "float32"),
+}
+SEMAPHORES = (["d_act", "d_x", "d_lst", "d_w1", "ms", "xqd", "lf8", "tr", "lc4", "of4", "ag4", "aqd", "bc4", "bqd", "hr4", "hqd",
+               "rc", "rs", "sent", "st0", "st1"]
+              + ["sg%d" % t for t in range(4)] + ["z%d" % b for b in range(4)] + ["yo%d" % o for o in range(4)]
+              + ["yc%d" % o for o in range(4)]
+              + ["x_%d" % s for s in range(4)] + ["h_%d" % s for s in range(4)]
+              + ["b0_%d" % s for s in range(4)] + ["b1_%d" % s for s in range(4)])
+
+
+def bits(es):
+    m = 0
+    for e in es:
+        m |= 1 << e
+    return m
+
+
+def ident(c):
+    a = topo_addr[0](c)
+    return DstId(rid=a[0], pnc=a[1])
+
+
+topo_addr = [None]
+
+
+def relays(me, others, topo):
+    far = [c for c in topo.cores_of(me) if topo.die(c) != topo.die(me) and all(topo.may_write(c, d) for d in others)]
+    across = [d for d in others if not topo.same_plane(topo.chip(me), topo.chip(d))]
+    return [(far[0], across), (far[1], [d for d in others if d not in across])]
+
+
+def rank_program(g, core, T, topo):
+    topo_addr[0] = topo.addr
+    rank = T.rank_of(core)
+    cores = list(T.cores)
+    n = len(cores)
+    sem = T.sem
+    u8 = dt.uint8
+
+    def copy(src, dsts, to, engines, rsem):
+        return RemoteDMATransfer(dst_ids=[ident(c) for c in to], dma_engine_mask=bits(engines), remote_sem=rsem,
+                                 srcs=[src], dsts=dsts)
+
+    if rank is None:
+        for s in range(n):
+            for c, to in relays(cores[s], [d for d in cores if d != cores[s]], topo):
+                if c == core:
+                    hand_on(g, core, s, to, T, topo, copy)
+        return
+
+    others = [(rank + k) % n for k in range(1, n)]
+    to = [cores[r] for r in others]
+    lo = topo.engines(core, to[0])
+    rel = relays(core, to, topo)
+    hi = [e for e in topo.engines(core, rel[0][0]) if e not in lo]
+
+    V, S, TE, SY = g.vector, g.scalar, g.tensor, g.sync
+
+    SY.dma_start(T.actb[:], T.act[:]).then_inc(sem.d_act, 16)
+    S.dma_start(T.xb[:], T.x[:]).then_inc(sem.d_x, 16)
+    SY.dma_start(T.w1b[:], T.w1[:]).then_inc(sem.d_w1, 16)
+    V.memset(T.lst[:], 0).then_inc(sem.ms, 1)
+    S.wait_ge(sem.ms, 1)
+    for q in range(4):
+        S.dma_start(T.lst[32 * q:32 * q + 8, :], T.act[:]).then_inc(sem.d_lst, 16)
+
+    g.wait_ge(sem.d_act, 16)
+    for t in range(4):
+        g.indirect_dma_start(T.w2g[:, 512 * t:512 * t + 512], None, T.w2[:],
+                             IndirectOffsetOnAxis(ap=T.actb[:, t:t + 1], axis=0),
+                             bounds_check=HU - 1).then_inc(sem["sg%d" % t], 16)
+    own = slice(T_ * rank, T_ * rank + T_)
+    g.wait_ge(sem.xqd, 1)
+    nsent = 0
+    g.remote_dma_fused([copy(T.xq[:, own].bitcast(u8), [T.xq[:, own].bitcast(u8)] * 3, to, lo, sem["x_%d" % rank])], local_sem=sem.sent)
+    g.remote_dma_fused([copy(T.xs[:, own], [T.xs[:, own]] * 3, to, lo, sem["x_%d" % rank])], local_sem=sem.sent)
+    nsent += 2 * len(lo)
+    g.wait_ge(sem.bqd, 1)
+    base = 512 * rank
+    rc = [c for c, _ in rel]
+    g.remote_dma_fused([copy(T.bq[:, 256:512].bitcast(u8), [T.rlq[:].bitcast(u8)] * 2, rc, hi, sem.rc),
+                        copy(T.bq[:, 0:256].bitcast(u8), [T.binq[:, base:base + 256].bitcast(u8)] * 3, to, lo, sem["b0_%d" % rank])],
+                       local_sem=sem.sent)
+    g.remote_dma_fused([copy(T.bs[:, 256:512], [T.rls[:]] * 2, rc, hi, sem.rs),
+                        copy(T.bs[:, 0:256], [T.bins[:, base:base + 256]] * 3, to, lo, sem["b0_%d" % rank])],
+                       local_sem=sem.sent)
+    nsent += 2 * (len(lo) + len(hi))
+    g.wait_ge(sem.hqd, 1)
+    w = 2
+    g.remote_dma_fused([copy(T.hq[:, T_ * r:T_ * r + T_].bitcast(u8), [T.hinq[:, own].bitcast(u8)], [cores[r]], lo[w * i:w * i + w],
+                             sem["h_%d" % rank]) for i, r in enumerate(others)], local_sem=sem.sent)
+    g.remote_dma_fused([copy(T.hs[:, T_ * r:T_ * r + T_], [T.hins[:, own]], [cores[r]], lo[w * i:w * i + w],
+                             sem["h_%d" % rank]) for i, r in enumerate(others)], local_sem=sem.sent)
+    nsent += 2 * 3 * w
+    g.wait_ge(sem.sent, nsent)
+
+    V.wait_ge(sem.d_x, 16)
+    V.quantize_mx(T.xq[:, own], T.xs[:, own], T.xb[:]).then_inc(sem.xqd, 1)
+    V.wait_ge(sem.d_lst, 64)
+    for b in range(4):
+        for h in range(2):
+            V.tensor_scalar(T.lf[:, 32 * b + 16 * h:32 * b + 16 * h + 16], T.lst[:, b:64:4], 4.0, None, AluOpType.mult).then_inc(sem.lf8, 1)
+    V.wait_ge(sem.lf8, 8)
+    V.transpose(T.lt[:], T.lf[:]).then_inc(sem.tr, 1)
+    V.wait_ge(sem.tr, 1)
+    for b in range(4):
+        V.tensor_copy(T.lc[:, 8 * b:8 * b + 8], T.lt[:, 32 * b:32 * b + 8]).then_inc(sem.lc4, 1)
+    V.wait_ge(sem.lc4, 4)
+    for t in range(4):
+        V.tensor_scalar(T.off[:, 32 * t:32 * t + 32], T.lc[:], float(t), None, AluOpType.add).then_inc(sem.of4, 1)
+    for t in range(4):
+        V.wait_ge(sem["sg%d" % t], 16)
+        V.tensor_copy(T.bb[:, t:2048:4], T.w2g[:, 512 * t:512 * t + 512]).then_inc(sem.bc4, 1)
+    V.wait_ge(sem.bc4, 4)
+    V.quantize_mx(T.bq[:], T.bs[:], T.bb[:]).then_inc(sem.bqd, 1)
+    V.wait_ge(sem.ag4, 4)
+    V.quantize_mx(T.aq[:], T.as_[:], T.ab[:]).then_inc(sem.aqd, 1)
+    for b in (1, 3):
+        V.wait_ge(sem["z%d" % b], 1)
+        V.tensor_scalar(T.hb[:, b:2048:4], T.zp[:, 512 * b:512 * b + 512], 0.05, 0.0, AluOpType.mult, AluOpType.max).then_inc(sem.hr4, 1)
+    V.wait_ge(sem.hr4, 4)
+    V.quantize_mx(T.hq[:], T.hs[:], T.hb[:]).then_inc(sem.hqd, 1)
+
+    S.wait_ge(sem.of4, 4)
+    S.wait_ge(sem.d_w1, 16)
+    for t in range(4):
+        S.activation(T.ab[:, t:2048:4], T.w1b[:, 0:4 * HU].indirect(T.off[:, 32 * t:32 * t + 32]),
+                     ActivationFunctionType.Copy).then_inc(sem.ag4, 1)
+    for b in (0, 2):
+        S.wait_ge(sem["z%d" % b], 1)
+        S.activation(T.hb[:, b:2048:4], T.zp[:, 512 * b:512 * b + 512], ActivationFunctionType.Relu, scale=0.05).then_inc(sem.hr4, 1)
+
+    TE.wait_ge(sem.xqd, 1)
+    TE.wait_ge(sem.aqd, 1)
+    for r in others:
+        TE.wait_ge(sem["x_%d" % r], 2 * len(lo))
+    for b in range(4):
+        TE.matmul_mx(T.zp[:, 512 * b:512 * b + 512], T.aq[:, 128 * b:128 * b + 128], T.as_[:, 128 * b:128 * b + 128],
+                     T.xq[:], T.xs[:], True, True).then_inc(sem["z%d" % b], 1)
+    TE.wait_ge(sem.bqd, 1)
+    TE.wait_ge(sem.hqd, 1)
+    for o in range(4):
+        TE.matmul_mx(T.yp[:, 512 * o:512 * o + 128], T.bq[:, 128 * o:128 * o + 128], T.bs[:, 128 * o:128 * o + 128],
+                     T.hq[:, own], T.hs[:, own], True, False)
+    for s in others:
+        TE.wait_ge(sem["h_%d" % s], 2 * w)
+    for half in range(2):
+        for s in others:
+            TE.wait_ge(sem["b%d_%d" % (half, s)], 2 * len(lo))
+            for o in (2 * half, 2 * half + 1):
+                a = 512 * s + 128 * o
+                last = s == others[-1]
+                m = TE.matmul_mx(T.yp[:, 512 * o:512 * o + 128], T.binq[:, a:a + 128], T.bins[:, a:a + 128],
+                                 T.hinq[:, T_ * s:T_ * s + T_], T.hins[:, T_ * s:T_ * s + T_], False, last)
+                if last:
+                    m.then_inc(sem["yo%d" % o], 1)
+
+    for half in range(2):
+        o = 2 * half
+        V.wait_ge(sem["yo%d" % o], 1)
+        V.tensor_copy(T.ysb[:, T_ * o:T_ * o + T_], T.yp[:, 512 * o:512 * o + 128]).then_inc(sem["yc%d" % o], 1)
+        SY.wait_ge(sem["yc%d" % o], 1)
+        SY.dma_start(T.y[:, T_ * o:T_ * o + T_], T.ysb[:, T_ * o:T_ * o + T_]).then_inc(sem.st0, 16)
+        o = 2 * half + 1
+        S.wait_ge(sem["yo%d" % o], 1)
+        S.activation(T.ysb[:, T_ * o:T_ * o + T_], T.yp[:, 512 * o:512 * o + 128], ActivationFunctionType.Copy).then_inc(sem["yc%d" % o], 1)
+        S.wait_ge(sem["yc%d" % o], 1)
+        S.dma_start(T.y[:, T_ * o:T_ * o + T_], T.ysb[:, T_ * o:T_ * o + T_]).then_inc(sem.st1, 16)
+    SY.wait_ge(sem.st0, 32)
+    S.wait_ge(sem.st1, 32)
+
+
+def hand_on(g, core, s, to, T, topo, copy):
+    sem = T.sem
+    lo = topo.engines(core, to[0])
+    me = T.cores[s]
+    fed = len([e for e in topo.engines(me, core) if e not in topo.engines(me, to[0])])
+    a = 512 * s + 256
+    g.wait_ge(sem.rc, fed)
+    g.remote_dma_fused([copy(T.rlq[:].bitcast(dt.uint8), [T.binq[:, a:a + 256].bitcast(dt.uint8)] * len(to), to, lo, sem["b1_%d" % s])],
+                       local_sem=sem.sent)
+    g.wait_ge(sem.rs, fed)
+    g.remote_dma_fused([copy(T.rls[:], [T.bins[:, a:a + 256]] * len(to), to, lo, sem["b1_%d" % s])], local_sem=sem.sent)
+    g.wait_ge(sem.sent, 2 * len(lo))

@@ -4,7 +4,10 @@ from concourse.mybir import dt, AluOpType, ActivationFunctionType
 T_ = 128
 HU = 1536
 ACT = 512
+NCORES = 112
 F8 = "float8_e4m3fn_x4"
+XP = T_ // 4
+X_AFTER = 0
 
 SCRATCH = {
     "actb": ("sbuf", [128, 4], "int32"),
@@ -25,17 +28,18 @@ SCRATCH = {
     "hq": ("sbuf", [128, 4 * T_], F8), "hs": ("sbuf", [128, 4 * T_], "uint8"),
     "hinq": ("sbuf", [128, 4 * T_], F8), "hins": ("sbuf", [128, 4 * T_], "uint8"),
     "binq": ("sbuf", [128, 4 * 512], F8), "bins": ("sbuf", [128, 4 * 512], "uint8"),
-    "rlq": ("sbuf", [128, 256], F8), "rls": ("sbuf", [128, 256], "uint8"),
+    "rlx": ("sbuf", [128, XP], F8), "rlq": ("sbuf", [128, 128], F8),
     "ysb": ("sbuf", [128, 4 * T_], "float32"),
     "zp": ("psum", [128, 2048], "float32"),
     "yp": ("psum", [128, 2048], "float32"),
 }
-SEMAPHORES = (["d_act", "d_x", "d_lst", "d_w1", "ms", "xqd", "lf8", "tr", "lc4", "of4", "ag4", "aqd", "bc4", "bqd", "hr4", "hqd",
-               "rc", "rs", "sent", "st0", "st1"]
-              + ["sg%d" % t for t in range(4)] + ["z%d" % b for b in range(4)] + ["yo%d" % o for o in range(4)]
-              + ["yc%d" % o for o in range(4)]
-              + ["x_%d" % s for s in range(4)] + ["h_%d" % s for s in range(4)]
-              + ["b0_%d" % s for s in range(4)] + ["b1_%d" % s for s in range(4)])
+SEMAPHORES = (["d_act", "d_x", "d_lst", "d_w1", "ms", "xqd", "lf8", "tr", "lc4", "of4", "ofa", "ag4", "aqd", "bc4", "bqd",
+               "rx", "rc", "sent", "st0", "st1"]
+              + ["sg%d" % t for t in range(4)] + ["z%d_%d" % (k, b) for k in range(4) for b in range(4)]
+              + ["hr%d" % k for k in range(4)] + ["hq%d" % k for k in range(4)]
+              + ["yo%d" % o for o in range(4)] + ["yc%d" % o for o in range(4)]
+              + ["x_%d" % s for s in range(4)] + ["h_%d" % s for s in range(4)] + ["s_%d" % s for s in range(4)]
+              + ["c_%d_%d" % (s, o) for s in range(4) for o in range(4)])
 
 
 def bits(es):
@@ -45,22 +49,35 @@ def bits(es):
     return m
 
 
-def ident(c):
-    a = topo_addr[0](c)
-    return DstId(rid=a[0], pnc=a[1])
+def slots(r, cores, topo):
+    rest = [(r + k) % len(cores) for k in range(1, len(cores))]
+    peer = [s for s in rest if topo.same_plane(topo.chip(cores[r]), topo.chip(cores[s]))]
+    return [s for s in rest if s not in peer] + peer + [r]
 
 
-topo_addr = [None]
+def relays(s, cores, topo):
+    me = cores[s]
+    to = [c for c in cores if c != me]
+    able = [c for c in range(NCORES) if c not in cores and all(topo.may_write(c, d) for d in to)]
+    near = [c for c in able if topo.chip(c) == topo.chip(me)]
+    peer = cores[slots(s, cores, topo)[2]]
+    far = [c for c in able if topo.mates(topo.chip(c), topo.chip(peer)) and topo.die(c) != topo.die(me)]
+    return [c for c in near if topo.die(c) == topo.die(me)][:1] + [c for c in near if topo.die(c) != topo.die(me)][:2] + far[:1]
 
 
-def relays(me, others, topo):
-    far = [c for c in topo.cores_of(me) if topo.die(c) != topo.die(me) and all(topo.may_write(c, d) for d in others)]
-    across = [d for d in others if not topo.same_plane(topo.chip(me), topo.chip(d))]
-    return [(far[0], across), (far[1], [d for d in others if d not in across])]
+def feeds(s, cores, topo):
+    rel = relays(s, cores, topo)
+    lo = topo.engines(cores[s], rel[3])
+    hi = [e for e in topo.engines(cores[s], rel[0]) if e not in lo]
+    return [hi[0:2], hi[2:4], hi[4:8], lo[0:4]], [hi, hi[0:4], hi[4:8], lo]
+
+
+def order(s, o, cores, topo):
+    rest = [(s + k) % len(cores) for k in range(1, len(cores))]
+    return rest[o % len(rest):] + rest[:o % len(rest)]
 
 
 def rank_program(g, core, T, topo):
-    topo_addr[0] = topo.addr
     rank = T.rank_of(core)
     cores = list(T.cores)
     n = len(cores)
@@ -68,122 +85,166 @@ def rank_program(g, core, T, topo):
     u8 = dt.uint8
 
     def copy(src, dsts, to, engines, rsem):
-        return RemoteDMATransfer(dst_ids=[ident(c) for c in to], dma_engine_mask=bits(engines), remote_sem=rsem,
-                                 srcs=[src], dsts=dsts)
+        ids = [DstId(rid=topo.addr(c)[0], pnc=topo.addr(c)[1]) for c in to]
+        return RemoteDMATransfer(dst_ids=ids, dma_engine_mask=bits(engines), remote_sem=rsem, srcs=[src], dsts=dsts)
+
+    def place(d, s):
+        return T_ * slots(d, cores, topo).index(s)
 
     if rank is None:
         for s in range(n):
-            for c, to in relays(cores[s], [d for d in cores if d != cores[s]], topo):
-                if c == core:
-                    hand_on(g, core, s, to, T, topo, copy)
+            rel = relays(s, cores, topo)
+            if core in rel:
+                hand_on(g, core, s, rel.index(core), T, topo, copy)
         return
 
+    sl = slots(rank, cores, topo)
+    cross, peer = sl[0:2], sl[2]
     others = [(rank + k) % n for k in range(1, n)]
-    to = [cores[r] for r in others]
-    lo = topo.engines(core, to[0])
-    rel = relays(core, to, topo)
-    hi = [e for e in topo.engines(core, rel[0][0]) if e not in lo]
+    lo = topo.engines(core, cores[peer])
+    rel = relays(rank, cores, topo)
+    fh, fb = feeds(rank, cores, topo)
+    own = slice(3 * T_, 4 * T_)
+    mine = slice(T_ * rank, T_ * rank + T_)
+    w = len(lo)
 
     V, S, TE, SY = g.vector, g.scalar, g.tensor, g.sync
 
     SY.dma_start(T.actb[:], T.act[:]).then_inc(sem.d_act, 16)
-    S.dma_start(T.xb[:], T.x[:]).then_inc(sem.d_x, 16)
+    S.dma_start(T.lst[0:8, :], T.act[:]).then_inc(sem.d_lst, 16)
+    SY.dma_start(T.xb[:], T.x[:]).then_inc(sem.d_x, 16)
     SY.dma_start(T.w1b[:], T.w1[:]).then_inc(sem.d_w1, 16)
-    V.memset(T.lst[:], 0).then_inc(sem.ms, 1)
-    S.wait_ge(sem.ms, 1)
-    for q in range(4):
-        S.dma_start(T.lst[32 * q:32 * q + 8, :], T.act[:]).then_inc(sem.d_lst, 16)
+
+    nsent = [0]
+
+    def send(transfers, engines):
+        g.remote_dma_fused(transfers, local_sem=sem.sent)
+        nsent[0] += engines
+
+    def send_x():
+        g.wait_ge(sem.xqd, 1)
+        ds = [peer] + cross
+        to = [cores[d] for d in ds]
+        send([copy(T.xs[:, own], [T.xs[:, place(d, rank):place(d, rank) + T_] for d in ds], to, lo, sem["x_%d" % rank])], w)
+        send([copy(T.xq[:, own].bitcast(u8), [T.xq[:, place(d, rank):place(d, rank) + T_].bitcast(u8) for d in ds],
+                   to, lo, sem["x_%d" % rank])], w)
+
+    def send_h():
+        k = w // 2
+        g.wait_ge(sem.hq2, 1)
+        pieces = [copy(T.hq[:, 2 * T_ + XP * i:2 * T_ + XP * i + XP].bitcast(u8), [T.rlx[:].bitcast(u8)], [rel[i]], fh[i], sem.rx)
+                  for i in range(4)]
+        plane = copy(T.hs[:, 2 * T_:3 * T_], [T.hins[:, mine]], [cores[peer]], lo[k:], sem["h_%d" % rank])
+        send(pieces + [plane], sum(len(e) for e in fh) + k)
+        g.wait_ge(sem.hq0, 1)
+        g.wait_ge(sem.hq1, 1)
+        send([copy(T.hq[:, T_ * i:T_ * i + T_].bitcast(u8), [T.hinq[:, mine].bitcast(u8)], [cores[d]],
+                   lo[k * i:k * i + k], sem["h_%d" % rank]) for i, d in enumerate(cross)], w)
+        send([copy(T.hs[:, T_ * i:T_ * i + T_], [T.hins[:, mine]], [cores[d]],
+                   lo[k * i:k * i + k], sem["h_%d" % rank]) for i, d in enumerate(cross)], w)
+
+    def feed(o):
+        return copy(T.bq[:, 128 * o:128 * o + 128].bitcast(u8), [T.rlq[:].bitcast(u8)], [rel[o]], fb[o], sem.rc)
 
     g.wait_ge(sem.d_act, 16)
     for t in range(4):
         g.indirect_dma_start(T.w2g[:, 512 * t:512 * t + 512], None, T.w2[:],
                              IndirectOffsetOnAxis(ap=T.actb[:, t:t + 1], axis=0),
                              bounds_check=HU - 1).then_inc(sem["sg%d" % t], 16)
-    own = slice(T_ * rank, T_ * rank + T_)
-    g.wait_ge(sem.xqd, 1)
-    nsent = 0
-    g.remote_dma_fused([copy(T.xq[:, own].bitcast(u8), [T.xq[:, own].bitcast(u8)] * 3, to, lo, sem["x_%d" % rank])], local_sem=sem.sent)
-    g.remote_dma_fused([copy(T.xs[:, own], [T.xs[:, own]] * 3, to, lo, sem["x_%d" % rank])], local_sem=sem.sent)
-    nsent += 2 * len(lo)
+        if t == X_AFTER:
+            send_x()
+    send_h()
     g.wait_ge(sem.bqd, 1)
-    base = 512 * rank
-    rc = [c for c, _ in rel]
-    g.remote_dma_fused([copy(T.bq[:, 256:512].bitcast(u8), [T.rlq[:].bitcast(u8)] * 2, rc, hi, sem.rc),
-                        copy(T.bq[:, 0:256].bitcast(u8), [T.binq[:, base:base + 256].bitcast(u8)] * 3, to, lo, sem["b0_%d" % rank])],
-                       local_sem=sem.sent)
-    g.remote_dma_fused([copy(T.bs[:, 256:512], [T.rls[:]] * 2, rc, hi, sem.rs),
-                        copy(T.bs[:, 0:256], [T.bins[:, base:base + 256]] * 3, to, lo, sem["b0_%d" % rank])],
-                       local_sem=sem.sent)
-    nsent += 2 * (len(lo) + len(hi))
-    g.wait_ge(sem.hqd, 1)
-    w = 2
-    g.remote_dma_fused([copy(T.hq[:, T_ * r:T_ * r + T_].bitcast(u8), [T.hinq[:, own].bitcast(u8)], [cores[r]], lo[w * i:w * i + w],
-                             sem["h_%d" % rank]) for i, r in enumerate(others)], local_sem=sem.sent)
-    g.remote_dma_fused([copy(T.hs[:, T_ * r:T_ * r + T_], [T.hins[:, own]], [cores[r]], lo[w * i:w * i + w],
-                             sem["h_%d" % rank]) for i, r in enumerate(others)], local_sem=sem.sent)
-    nsent += 2 * 3 * w
-    g.wait_ge(sem.sent, nsent)
+    send([feed(o) for o in (3, 1, 2)], 2 * w)
+    send([feed(0), copy(T.bs[:], [T.bins[:, 512 * rank:512 * rank + 512]] * 3, [cores[d] for d in others], lo, sem["s_%d" % rank])], 2 * w)
+    g.wait_ge(sem.sent, nsent[0])
 
-    V.wait_ge(sem.d_x, 16)
-    V.quantize_mx(T.xq[:, own], T.xs[:, own], T.xb[:]).then_inc(sem.xqd, 1)
-    V.wait_ge(sem.d_lst, 64)
+    V.memset(T.lf[0:32, :], 0.0).then_inc(sem.ms, 1)
+    V.wait_ge(sem.ms, 1)
+    V.wait_ge(sem.d_lst, 16)
     for b in range(4):
         for h in range(2):
-            V.tensor_scalar(T.lf[:, 32 * b + 16 * h:32 * b + 16 * h + 16], T.lst[:, b:64:4], 4.0, None, AluOpType.mult).then_inc(sem.lf8, 1)
+            V.tensor_scalar(T.lf[0:8, 32 * b + 16 * h:32 * b + 16 * h + 16], T.lst[0:8, b:64:4], 4.0, None, AluOpType.mult).then_inc(sem.lf8, 1)
+    V.wait_ge(sem.d_x, 16)
+    V.quantize_mx(T.xq[:, own], T.xs[:, own], T.xb[:]).then_inc(sem.xqd, 1)
     V.wait_ge(sem.lf8, 8)
-    V.transpose(T.lt[:], T.lf[:]).then_inc(sem.tr, 1)
+    V.transpose(T.lt[0:32, :], T.lf[0:32, :]).then_inc(sem.tr, 1)
     V.wait_ge(sem.tr, 1)
     for b in range(4):
-        V.tensor_copy(T.lc[:, 8 * b:8 * b + 8], T.lt[:, 32 * b:32 * b + 8]).then_inc(sem.lc4, 1)
+        V.tensor_copy(T.lc[0:32, 8 * b:8 * b + 8], T.lt[0:32, 32 * b:32 * b + 8]).then_inc(sem.lc4, 1)
     V.wait_ge(sem.lc4, 4)
     for t in range(4):
-        V.tensor_scalar(T.off[:, 32 * t:32 * t + 32], T.lc[:], float(t), None, AluOpType.add).then_inc(sem.of4, 1)
-    for t in range(4):
-        V.wait_ge(sem["sg%d" % t], 16)
-        V.tensor_copy(T.bb[:, t:2048:4], T.w2g[:, 512 * t:512 * t + 512]).then_inc(sem.bc4, 1)
-    V.wait_ge(sem.bc4, 4)
-    V.quantize_mx(T.bq[:], T.bs[:], T.bb[:]).then_inc(sem.bqd, 1)
-    V.wait_ge(sem.ag4, 4)
-    V.quantize_mx(T.aq[:], T.as_[:], T.ab[:]).then_inc(sem.aqd, 1)
-    for b in (1, 3):
-        V.wait_ge(sem["z%d" % b], 1)
-        V.tensor_scalar(T.hb[:, b:2048:4], T.zp[:, 512 * b:512 * b + 512], 0.05, 0.0, AluOpType.mult, AluOpType.max).then_inc(sem.hr4, 1)
-    V.wait_ge(sem.hr4, 4)
-    V.quantize_mx(T.hq[:], T.hs[:], T.hb[:]).then_inc(sem.hqd, 1)
-
-    S.wait_ge(sem.of4, 4)
+        V.tensor_scalar(T.off[0:32, 32 * t:32 * t + 32], T.lc[0:32, :], float(t), None, AluOpType.add).then_inc(sem.of4, 1)
+    V.wait_ge(sem.of4, 4)
+    for q in range(1, 4):
+        V.tensor_copy(T.off[32 * q:32 * q + 32, :], T.off[0:32, :]).then_inc(sem.ofa, 1)
+    V.wait_ge(sem.ofa, 3)
+    S.wait_ge(sem.ofa, 3)
+    V.wait_ge(sem.d_w1, 16)
     S.wait_ge(sem.d_w1, 16)
     for t in range(4):
-        S.activation(T.ab[:, t:2048:4], T.w1b[:, 0:4 * HU].indirect(T.off[:, 32 * t:32 * t + 32]),
-                     ActivationFunctionType.Copy).then_inc(sem.ag4, 1)
-    for b in (0, 2):
-        S.wait_ge(sem["z%d" % b], 1)
-        S.activation(T.hb[:, b:2048:4], T.zp[:, 512 * b:512 * b + 512], ActivationFunctionType.Relu, scale=0.05).then_inc(sem.hr4, 1)
+        win = T.w1b[:, 0:4 * HU].indirect(T.off[:, 32 * t:32 * t + 32])
+        if t < 2:
+            S.activation(T.ab[:, t:2048:4], win, ActivationFunctionType.Copy).then_inc(sem.ag4, 1)
+        else:
+            V.tensor_copy(T.ab[:, t:2048:4], win).then_inc(sem.ag4, 1)
+    V.wait_ge(sem.ag4, 4)
+    V.quantize_mx(T.aq[:], T.as_[:], T.ab[:]).then_inc(sem.aqd, 1)
+
+    def spread(t):
+        V.wait_ge(sem["sg%d" % t], 16)
+        V.tensor_copy(T.bb[:, t:2048:4], T.w2g[:, 512 * t:512 * t + 512]).then_inc(sem.bc4, 1)
 
     TE.wait_ge(sem.xqd, 1)
     TE.wait_ge(sem.aqd, 1)
-    for r in others:
-        TE.wait_ge(sem["x_%d" % r], 2 * len(lo))
-    for b in range(4):
-        TE.matmul_mx(T.zp[:, 512 * b:512 * b + 512], T.aq[:, 128 * b:128 * b + 128], T.as_[:, 128 * b:128 * b + 128],
-                     T.xq[:], T.xs[:], True, True).then_inc(sem["z%d" % b], 1)
+    arrival = [3, 2] + sorted(range(2), key=lambda k: slots(sl[k], cores, topo).index(rank))
+    spread(0)
+    for i, k in enumerate(arrival):
+        ps = T.yp if i % 2 else T.zp
+        cols = slice(T_ * k, T_ * k + T_)
+        if sl[k] != rank:
+            TE.wait_ge(sem["x_%d" % sl[k]], 2 * w)
+        if i >= 2:
+            TE.wait_ge(sem["hr%d" % arrival[i - 2]], 4)
+        for b in range(4):
+            TE.matmul_mx(ps[:, 512 * b:512 * b + T_], T.aq[:, 128 * b:128 * b + 128], T.as_[:, 128 * b:128 * b + 128],
+                         T.xq[:, cols], T.xs[:, cols], True, True).then_inc(sem["z%d_%d" % (k, b)], 1)
+            dst, src = T.hb[:, 4 * T_ * k + b:4 * T_ * k + 4 * T_:4], ps[:, 512 * b:512 * b + T_]
+            if b % 2:
+                V.wait_ge(sem["z%d_%d" % (k, b)], 1)
+                V.tensor_scalar(dst, src, 0.05, 0.0, AluOpType.mult, AluOpType.max).then_inc(sem["hr%d" % k], 1)
+            else:
+                S.wait_ge(sem["z%d_%d" % (k, b)], 1)
+                S.activation(dst, src, ActivationFunctionType.Relu, scale=0.05).then_inc(sem["hr%d" % k], 1)
+        V.wait_ge(sem["hr%d" % k], 4)
+        V.quantize_mx(T.hq[:, cols], T.hs[:, cols], T.hb[:, 4 * T_ * k:4 * T_ * k + 4 * T_]).then_inc(sem["hq%d" % k], 1)
+        if i == 1:
+            spread(1)
+    for t in range(2, 4):
+        spread(t)
+    V.wait_ge(sem.bc4, 4)
+    V.quantize_mx(T.bq[:], T.bs[:], T.bb[:]).then_inc(sem.bqd, 1)
+
     TE.wait_ge(sem.bqd, 1)
-    TE.wait_ge(sem.hqd, 1)
+    TE.wait_ge(sem.hq3, 1)
+    TE.wait_ge(sem["hr%d" % arrival[3]], 4)
     for o in range(4):
         TE.matmul_mx(T.yp[:, 512 * o:512 * o + 128], T.bq[:, 128 * o:128 * o + 128], T.bs[:, 128 * o:128 * o + 128],
                      T.hq[:, own], T.hs[:, own], True, False)
-    for s in others:
-        TE.wait_ge(sem["h_%d" % s], 2 * w)
-    for half in range(2):
-        for s in others:
-            TE.wait_ge(sem["b%d_%d" % (half, s)], 2 * len(lo))
-            for o in (2 * half, 2 * half + 1):
-                a = 512 * s + 128 * o
-                last = s == others[-1]
-                m = TE.matmul_mx(T.yp[:, 512 * o:512 * o + 128], T.binq[:, a:a + 128], T.bins[:, a:a + 128],
-                                 T.hinq[:, T_ * s:T_ * s + T_], T.hins[:, T_ * s:T_ * s + T_], False, last)
-                if last:
-                    m.then_inc(sem["yo%d" % o], 1)
+    parts = sorted([(order(s, o, cores, topo).index(rank), o, s) for s in others for o in range(4)])
+    seen, left = [], [3] * 4
+    for _, o, s in parts:
+        if s not in seen:
+            seen.append(s)
+            TE.wait_ge(sem["s_%d" % s], w)
+            TE.wait_ge(sem["h_%d" % s], w // 2 + 4 * w if s == peer else w)
+        TE.wait_ge(sem["c_%d_%d" % (s, o)], w)
+        left[o] -= 1
+        a = 512 * s + 128 * o
+        m = TE.matmul_mx(T.yp[:, 512 * o:512 * o + 128], T.binq[:, a:a + 128], T.bins[:, a:a + 128],
+                         T.hinq[:, T_ * s:T_ * s + T_], T.hins[:, T_ * s:T_ * s + T_], False, left[o] == 0)
+        if left[o] == 0:
+            m.then_inc(sem["yo%d" % o], 1)
 
     for half in range(2):
         o = 2 * half
@@ -200,15 +261,19 @@ def rank_program(g, core, T, topo):
     S.wait_ge(sem.st1, 32)
 
 
-def hand_on(g, core, s, to, T, topo, copy):
+def hand_on(g, core, s, o, T, topo, copy):
     sem = T.sem
-    lo = topo.engines(core, to[0])
-    me = T.cores[s]
-    fed = len([e for e in topo.engines(me, core) if e not in topo.engines(me, to[0])])
-    a = 512 * s + 256
-    g.wait_ge(sem.rc, fed)
-    g.remote_dma_fused([copy(T.rlq[:].bitcast(dt.uint8), [T.binq[:, a:a + 256].bitcast(dt.uint8)] * len(to), to, lo, sem["b1_%d" % s])],
+    cores = list(T.cores)
+    peer = slots(s, cores, topo)[2]
+    lo = topo.engines(core, cores[peer])
+    fh, fb = feeds(s, cores, topo)
+    a = T_ * s + XP * o
+    g.wait_ge(sem.rx, len(fh[o]))
+    g.remote_dma_fused([copy(T.rlx[:].bitcast(dt.uint8), [T.hinq[:, a:a + XP].bitcast(dt.uint8)], [cores[peer]], lo, sem["h_%d" % s])],
                        local_sem=sem.sent)
-    g.wait_ge(sem.rs, fed)
-    g.remote_dma_fused([copy(T.rls[:], [T.bins[:, a:a + 256]] * len(to), to, lo, sem["b1_%d" % s])], local_sem=sem.sent)
+    to = [cores[d] for d in order(s, o, cores, topo)]
+    a = 512 * s + 128 * o
+    g.wait_ge(sem.rc, len(fb[o]))
+    g.remote_dma_fused([copy(T.rlq[:].bitcast(dt.uint8), [T.binq[:, a:a + 128].bitcast(dt.uint8)] * len(to), to, lo, sem["c_%d_%d" % (s, o)])],
+                       local_sem=sem.sent)
     g.wait_ge(sem.sent, 2 * len(lo))

@@ -28,13 +28,13 @@ SCRATCH = {
     "hq": ("sbuf", [128, 4 * T_], F8), "hs": ("sbuf", [128, 4 * T_], "uint8"),
     "hinq": ("sbuf", [128, 4 * T_], F8), "hins": ("sbuf", [128, 4 * T_], "uint8"),
     "binq": ("sbuf", [128, 4 * 512], F8), "bins": ("sbuf", [128, 4 * 512], "uint8"),
-    "rlx": ("sbuf", [128, XP], F8), "rlq": ("sbuf", [128, 128], F8),
+    "rlx": ("sbuf", [128, XP], F8), "rlq": ("sbuf", [128, 128], F8), "rlh": ("sbuf", [128, T_], F8),
     "ysb": ("sbuf", [128, 4 * T_], "float32"),
     "zp": ("psum", [128, 2048], "float32"),
     "yp": ("psum", [128, 2048], "float32"),
 }
-SEMAPHORES = (["d_act", "d_x", "d_lst", "d_w1", "ms", "xqd", "lf8", "tr", "lc4", "of4", "ofa", "ag4", "aqd", "bc4", "bqd",
-               "rx", "rc", "sent", "st0", "st1"]
+SEMAPHORES = (["d_act", "d_x", "d_lst", "d_w1", "ms", "xqd", "lf8", "tr", "lc4", "of4", "ofa", "ag4", "aqd", "bc4", "bc1", "bc2", "bq0", "bq1", "bq2",
+               "rx", "rc", "rh", "sent", "st0", "st1"]
               + ["sg%d" % t for t in range(4)] + ["z%d_%d" % (k, b) for k in range(4) for b in range(4)]
               + ["hr%d" % k for k in range(4)] + ["hq%d" % k for k in range(4)]
               + ["yo%d" % o for o in range(4)] + ["yc%d" % o for o in range(4)]
@@ -61,7 +61,7 @@ def relays(s, cores, topo):
     able = [c for c in range(NCORES) if c not in cores and all(topo.may_write(c, d) for d in to)]
     near = [c for c in able if topo.chip(c) == topo.chip(me)]
     peer = cores[slots(s, cores, topo)[2]]
-    far = [c for c in able if topo.mates(topo.chip(c), topo.chip(peer)) and topo.die(c) != topo.die(me)]
+    far = [c for c in able if topo.mates(topo.chip(c), topo.chip(peer)) and topo.die(c) == topo.die(me)]
     return [c for c in near if topo.die(c) == topo.die(me)][:1] + [c for c in near if topo.die(c) != topo.die(me)][:2] + far[:1]
 
 
@@ -107,6 +107,7 @@ def rank_program(g, core, T, topo):
     own = slice(3 * T_, 4 * T_)
     mine = slice(T_ * rank, T_ * rank + T_)
     w = len(lo)
+    ex = lo
 
     V, S, TE, SY = g.vector, g.scalar, g.tensor, g.sync
 
@@ -125,9 +126,9 @@ def rank_program(g, core, T, topo):
         g.wait_ge(sem.xqd, 1)
         ds = [peer] + cross
         to = [cores[d] for d in ds]
-        send([copy(T.xs[:, own], [T.xs[:, place(d, rank):place(d, rank) + T_] for d in ds], to, lo, sem["x_%d" % rank])], w)
+        send([copy(T.xs[:, own], [T.xs[:, place(d, rank):place(d, rank) + T_] for d in ds], to, ex, sem["x_%d" % rank])], len(ex))
         send([copy(T.xq[:, own].bitcast(u8), [T.xq[:, place(d, rank):place(d, rank) + T_].bitcast(u8) for d in ds],
-                   to, lo, sem["x_%d" % rank])], w)
+                   to, ex, sem["x_%d" % rank])], len(ex))
 
     def send_h():
         k = w // 2
@@ -138,8 +139,7 @@ def rank_program(g, core, T, topo):
         send(pieces + [plane], sum(len(e) for e in fh) + k)
         g.wait_ge(sem.hq0, 1)
         g.wait_ge(sem.hq1, 1)
-        send([copy(T.hq[:, T_ * i:T_ * i + T_].bitcast(u8), [T.hinq[:, mine].bitcast(u8)], [cores[d]],
-                   lo[k * i:k * i + k], sem["h_%d" % rank]) for i, d in enumerate(cross)], w)
+        send([copy(T.hq[:, T_ * i:T_ * i + T_].bitcast(u8), [T.rlh[:].bitcast(u8)], [rel[1 + i]], fb[1 + i], sem.rh) for i in range(2)], w)
         send([copy(T.hs[:, T_ * i:T_ * i + T_], [T.hins[:, mine]], [cores[d]],
                    lo[k * i:k * i + k], sem["h_%d" % rank]) for i, d in enumerate(cross)], w)
 
@@ -154,8 +154,11 @@ def rank_program(g, core, T, topo):
         if t == X_AFTER:
             send_x()
     send_h()
-    g.wait_ge(sem.bqd, 1)
-    send([feed(o) for o in (3, 1, 2)], 2 * w)
+    g.wait_ge(sem.bq0, 1)
+    send([feed(3)], w)
+    g.wait_ge(sem.bq1, 1)
+    send([feed(1), feed(2)], w)
+    g.wait_ge(sem.bq2, 1)
     send([feed(0), copy(T.bs[:], [T.bins[:, 512 * rank:512 * rank + 512]] * 3, [cores[d] for d in others], lo, sem["s_%d" % rank])], 2 * w)
     g.wait_ge(sem.sent, nsent[0])
 
@@ -197,13 +200,27 @@ def rank_program(g, core, T, topo):
 
     TE.wait_ge(sem.xqd, 1)
     TE.wait_ge(sem.aqd, 1)
-    arrival = [3, 2] + sorted(range(2), key=lambda k: slots(sl[k], cores, topo).index(rank))
+    arrival = [2] + sorted(range(2), key=lambda k: slots(sl[k], cores, topo).index(rank)) + [3]
     spread(0)
     for i, k in enumerate(arrival):
         ps = T.yp if i % 2 else T.zp
         cols = slice(T_ * k, T_ * k + T_)
         if sl[k] != rank:
-            TE.wait_ge(sem["x_%d" % sl[k]], 2 * w)
+            TE.wait_ge(sem["x_%d" % sl[k]], 2 * len(ex))
+        else:
+            for t in range(1, 3):
+                spread(t)
+            V.wait_ge(sem.sg3, 16)
+            V.tensor_copy(T.bb[:, 1536 + 3:2048:4], T.w2g[:, 1536 + 384:2048]).then_inc(sem.bc4, 1)
+            S.wait_ge(sem.sg3, 16)
+            S.activation(T.bb[:, 512 + 3:1536:4], T.w2g[:, 1536 + 128:1536 + 384], ActivationFunctionType.Copy).then_inc(sem.bc1, 1)
+            S.activation(T.bb[:, 3:512:4], T.w2g[:, 1536:1536 + 128], ActivationFunctionType.Copy).then_inc(sem.bc2, 1)
+            V.wait_ge(sem.bc4, 4)
+            V.quantize_mx(T.bq[:, 384:512], T.bs[:, 384:512], T.bb[:, 1536:2048]).then_inc(sem.bq0, 1)
+            V.wait_ge(sem.bc1, 1)
+            V.quantize_mx(T.bq[:, 128:384], T.bs[:, 128:384], T.bb[:, 512:1536]).then_inc(sem.bq1, 1)
+            V.wait_ge(sem.bc2, 1)
+            V.quantize_mx(T.bq[:, 0:128], T.bs[:, 0:128], T.bb[:, 0:512]).then_inc(sem.bq2, 1)
         if i >= 2:
             TE.wait_ge(sem["hr%d" % arrival[i - 2]], 4)
         for b in range(4):
@@ -218,14 +235,9 @@ def rank_program(g, core, T, topo):
                 S.activation(dst, src, ActivationFunctionType.Relu, scale=0.05).then_inc(sem["hr%d" % k], 1)
         V.wait_ge(sem["hr%d" % k], 4)
         V.quantize_mx(T.hq[:, cols], T.hs[:, cols], T.hb[:, 4 * T_ * k:4 * T_ * k + 4 * T_]).then_inc(sem["hq%d" % k], 1)
-        if i == 1:
-            spread(1)
-    for t in range(2, 4):
-        spread(t)
-    V.wait_ge(sem.bc4, 4)
-    V.quantize_mx(T.bq[:], T.bs[:], T.bb[:]).then_inc(sem.bqd, 1)
 
-    TE.wait_ge(sem.bqd, 1)
+    for j in range(3):
+        TE.wait_ge(sem["bq%d" % j], 1)
     TE.wait_ge(sem.hq3, 1)
     TE.wait_ge(sem["hr%d" % arrival[3]], 4)
     for o in range(4):
@@ -237,7 +249,7 @@ def rank_program(g, core, T, topo):
         if s not in seen:
             seen.append(s)
             TE.wait_ge(sem["s_%d" % s], w)
-            TE.wait_ge(sem["h_%d" % s], w // 2 + 4 * w if s == peer else w)
+            TE.wait_ge(sem["h_%d" % s], w // 2 + (4 * w if s == peer else w))
         TE.wait_ge(sem["c_%d_%d" % (s, o)], w)
         left[o] -= 1
         a = 512 * s + 128 * o
@@ -271,9 +283,16 @@ def hand_on(g, core, s, o, T, topo, copy):
     g.wait_ge(sem.rx, len(fh[o]))
     g.remote_dma_fused([copy(T.rlx[:].bitcast(dt.uint8), [T.hinq[:, a:a + XP].bitcast(dt.uint8)], [cores[peer]], lo, sem["h_%d" % s])],
                        local_sem=sem.sent)
+    calls = 2
+    if o in (1, 2):
+        d = slots(s, cores, topo)[o - 1]
+        g.wait_ge(sem.rh, len(fb[o]))
+        g.remote_dma_fused([copy(T.rlh[:].bitcast(dt.uint8), [T.hinq[:, T_ * s:T_ * s + T_].bitcast(dt.uint8)], [cores[d]], lo, sem["h_%d" % s])],
+                           local_sem=sem.sent)
+        calls = 3
     to = [cores[d] for d in order(s, o, cores, topo)]
     a = 512 * s + 128 * o
     g.wait_ge(sem.rc, len(fb[o]))
     g.remote_dma_fused([copy(T.rlq[:].bitcast(dt.uint8), [T.binq[:, a:a + 128].bitcast(dt.uint8)] * len(to), to, lo, sem["c_%d_%d" % (s, o)])],
                        local_sem=sem.sent)
-    g.wait_ge(sem.sent, 2 * len(lo))
+    g.wait_ge(sem.sent, calls * len(lo))

@@ -28,18 +28,21 @@ SCRATCH = {
     "hq": ("sbuf", [128, 4 * T_], F8), "hs": ("sbuf", [128, 4 * T_], "uint8"),
     "hinq": ("sbuf", [128, 4 * T_], F8), "hins": ("sbuf", [128, 4 * T_], "uint8"),
     "binq": ("sbuf", [128, 4 * 512], F8), "bins": ("sbuf", [128, 4 * 512], "uint8"),
-    "rlx": ("sbuf", [128, XP], F8), "rlq": ("sbuf", [128, 128], F8), "rlh": ("sbuf", [128, T_], F8),
+    "rlx": ("sbuf", [128, XP], F8), "rlh": ("sbuf", [128, 2 * T_], F8),
+    "rlp": ("sbuf", [128, 2 * T_], "uint8"), "rlq": ("sbuf", [128, 4 * 128], F8),
     "ysb": ("sbuf", [128, 4 * T_], "float32"),
     "zp": ("psum", [128, 2048], "float32"),
     "yp": ("psum", [128, 2048], "float32"),
 }
-SEMAPHORES = (["d_act", "d_x", "d_lst", "d_w1", "ms", "xqd", "lf8", "tr", "lc4", "of4", "ofa", "ag4", "aqd", "bc4", "bc1", "bc2", "bq0", "bq1", "bq2",
-               "rx", "rc", "rh", "sent", "st0", "st1"]
+SEMAPHORES = (["d_act", "d_x", "d_lst", "d_w1", "ms", "xqd", "lf8", "tr", "lc4", "of4", "ofa", "ag4", "aqd", "bc4",
+               "rx", "rh0", "rh1", "sent", "st0", "st1"]
+              + ["bc%d" % o for o in range(4)] + ["bq%d" % o for o in range(4)] + ["rc%d" % s for s in range(4)]
               + ["sg%d" % t for t in range(4)] + ["z%d_%d" % (k, b) for k in range(4) for b in range(4)]
               + ["hr%d" % k for k in range(4)] + ["hq%d" % k for k in range(4)]
               + ["yo%d" % o for o in range(4)] + ["yc%d" % o for o in range(4)]
               + ["x_%d" % s for s in range(4)] + ["h_%d" % s for s in range(4)] + ["s_%d" % s for s in range(4)]
               + ["c_%d_%d" % (s, o) for s in range(4) for o in range(4)])
+BX, BY, BZ, BW = 3, 2, 1, 0
 
 
 def bits(es):
@@ -55,26 +58,36 @@ def slots(r, cores, topo):
     return [s for s in rest if s not in peer] + peer + [r]
 
 
-def relays(s, cores, topo):
+def arrival(r, cores, topo):
+    sl = slots(r, cores, topo)
+    return [2] + sorted(range(2), key=lambda k: slots(sl[k], cores, topo).index(r)) + [3]
+
+
+def dests(s, cores, topo):
+    sl = slots(s, cores, topo)
+    return [sl[k] for k in arrival(s, cores, topo)[0:3]]
+
+
+def helpers(s, cores, topo):
     me = cores[s]
-    to = [c for c in cores if c != me]
-    able = [c for c in range(NCORES) if c not in cores and all(topo.may_write(c, d) for d in to)]
-    near = [c for c in able if topo.chip(c) == topo.chip(me)]
-    peer = cores[slots(s, cores, topo)[2]]
-    far = [c for c in able if topo.mates(topo.chip(c), topo.chip(peer)) and topo.die(c) == topo.die(me)]
-    return [c for c in near if topo.die(c) == topo.die(me)][:1] + [c for c in near if topo.die(c) != topo.die(me)][:2] + far[:1]
+    near = [c for c in topo.cores_of(me) if c != me]
+    able = [c for c in near if all(topo.may_write(c, d) for d in cores)]
+    rest = [c for c in near if c not in able]
+    mate = [c for c in range(NCORES) if topo.mates(topo.chip(c), topo.chip(me)) and topo.may_write(c, me)]
+
+    def on(cs, same):
+        return [c for c in cs if (topo.die(c) == topo.die(me)) == same]
+
+    return {"n1": on(able, True)[0], "n0a": on(able, False)[0], "n0b": on(able, False)[1],
+            "f1": on(rest, True)[0], "f0": on(rest, False)[0], "m1": on(mate, True)[0], "m0": on(mate, False)[0]}
 
 
-def feeds(s, cores, topo):
-    rel = relays(s, cores, topo)
-    lo = topo.engines(cores[s], rel[3])
-    hi = [e for e in topo.engines(cores[s], rel[0]) if e not in lo]
-    return [hi[0:2], hi[2:4], hi[4:8], lo[0:4]], [hi, hi[0:4], hi[4:8], lo]
+def engines(s, cores, topo):
+    lo = topo.engines(cores[s], cores[(s + 1) % len(cores)])
+    return lo, [e for e in topo.engines(cores[s], helpers(s, cores, topo)["n1"]) if e not in lo]
 
 
-def order(s, o, cores, topo):
-    rest = [(s + k) % len(cores) for k in range(1, len(cores))]
-    return rest[o % len(rest):] + rest[:o % len(rest)]
+PARTS = ["f0", "n0b", "f1", "n0a"]
 
 
 def rank_program(g, core, T, topo):
@@ -93,19 +106,19 @@ def rank_program(g, core, T, topo):
 
     if rank is None:
         for s in range(n):
-            rel = relays(s, cores, topo)
-            if core in rel:
-                hand_on(g, core, s, rel.index(core), T, topo, copy)
+            for role, c in helpers(s, cores, topo).items():
+                if c == core:
+                    hand_on(g, core, s, role, T, topo, copy)
         return
 
     sl = slots(rank, cores, topo)
-    cross, peer = sl[0:2], sl[2]
-    others = [(rank + k) % n for k in range(1, n)]
-    lo = topo.engines(core, cores[peer])
-    rel = relays(rank, cores, topo)
-    fh, fb = feeds(rank, cores, topo)
+    arr = arrival(rank, cores, topo)
+    cross = sl[0:2]
+    peer, ca, cb = dests(rank, cores, topo)
+    hp = helpers(rank, cores, topo)
+    lo, hi = engines(rank, cores, topo)
+    every = lo + hi
     own = slice(3 * T_, 4 * T_)
-    mine = slice(T_ * rank, T_ * rank + T_)
     w = len(lo)
     ex = lo
 
@@ -118,33 +131,40 @@ def rank_program(g, core, T, topo):
 
     nsent = [0]
 
-    def send(transfers, engines):
-        g.remote_dma_fused(transfers, local_sem=sem.sent)
-        nsent[0] += engines
+    def send(*moves):
+        g.remote_dma_fused([copy(*m) for m in moves], local_sem=sem.sent)
+        nsent[0] += sum(len(m[3]) for m in moves)
 
     def send_x():
         g.wait_ge(sem.xqd, 1)
         ds = [peer] + cross
         to = [cores[d] for d in ds]
-        send([copy(T.xs[:, own], [T.xs[:, place(d, rank):place(d, rank) + T_] for d in ds], to, ex, sem["x_%d" % rank])], len(ex))
-        send([copy(T.xq[:, own].bitcast(u8), [T.xq[:, place(d, rank):place(d, rank) + T_].bitcast(u8) for d in ds],
-                   to, ex, sem["x_%d" % rank])], len(ex))
+        send((T.xs[:, own], [T.xs[:, place(d, rank):place(d, rank) + T_] for d in ds], to, ex, sem["x_%d" % rank]))
+        send((T.xq[:, own].bitcast(u8), [T.xq[:, place(d, rank):place(d, rank) + T_].bitcast(u8) for d in ds], to, ex, sem["x_%d" % rank]))
 
     def send_h():
-        k = w // 2
         g.wait_ge(sem.hq2, 1)
-        pieces = [copy(T.hq[:, 2 * T_ + XP * i:2 * T_ + XP * i + XP].bitcast(u8), [T.rlx[:].bitcast(u8)], [rel[i]], fh[i], sem.rx)
-                  for i in range(4)]
-        plane = copy(T.hs[:, 2 * T_:3 * T_], [T.hins[:, mine]], [cores[peer]], lo[k:], sem["h_%d" % rank])
-        send(pieces + [plane], sum(len(e) for e in fh) + k)
-        g.wait_ge(sem.hq0, 1)
-        g.wait_ge(sem.hq1, 1)
-        send([copy(T.hq[:, T_ * i:T_ * i + T_].bitcast(u8), [T.rlh[:].bitcast(u8)], [rel[1 + i]], fb[1 + i], sem.rh) for i in range(2)], w)
-        send([copy(T.hs[:, T_ * i:T_ * i + T_], [T.hins[:, mine]], [cores[d]],
-                   lo[k * i:k * i + k], sem["h_%d" % rank]) for i, d in enumerate(cross)], w)
+        for pair in ((0, 1), (2, 3)):
+            send(*[(T.hq[:, 2 * T_ + XP * i:2 * T_ + XP * i + XP].bitcast(u8), [T.rlx[:].bitcast(u8)], [hp[PARTS[i]]],
+                    every[4 * i:4 * i + 4], sem.rx) for i in pair])
+        send((T.hs[:, 2 * T_:3 * T_], [T.rlp[:, 0:T_]], [hp["n1"]], every, sem.rx))
 
-    def feed(o):
-        return copy(T.bq[:, 128 * o:128 * o + 128].bitcast(u8), [T.rlq[:].bitcast(u8)], [rel[o]], fb[o], sem.rc)
+    def send_cross():
+        far = helpers(ca, cores, topo)
+        for i, (k, rp, rq, e) in enumerate(((arr[1], far["m0"], far["m1"], lo), (arr[2], hp["n1"], hp["n0b"], hi))):
+            g.wait_ge(sem["hq%d" % k], 1)
+            send((T.hs[:, T_ * k:T_ * k + T_], [T.rlp[:, T_:2 * T_]], [rp], e, sem["rh%d" % i]))
+            send((T.hq[:, T_ * k:T_ * k + T_].bitcast(u8), [T.rlh[:, T_ * i:T_ * i + T_].bitcast(u8)], [rq], e, sem["rh%d" % i]))
+
+    def block(o):
+        return T.bq[:, 128 * o:128 * o + 128].bitcast(u8)
+
+    def feed(o, role, e):
+        return block(o), [T.rlq[:, 128 * rank:128 * rank + 128].bitcast(u8)], [hp[role]], e, sem["rc%d" % rank]
+
+    def direct(o):
+        a = 512 * rank + 128 * o
+        return block(o), [T.binq[:, a:a + 128].bitcast(u8)], [cores[peer]], lo, sem["c_%d_%d" % (rank, o)]
 
     g.wait_ge(sem.d_act, 16)
     for t in range(4):
@@ -154,12 +174,17 @@ def rank_program(g, core, T, topo):
         if t == X_AFTER:
             send_x()
     send_h()
-    g.wait_ge(sem.bq0, 1)
-    send([feed(3)], w)
-    g.wait_ge(sem.bq1, 1)
-    send([feed(1), feed(2)], w)
-    g.wait_ge(sem.bq2, 1)
-    send([feed(0), copy(T.bs[:], [T.bins[:, 512 * rank:512 * rank + 512]] * 3, [cores[d] for d in others], lo, sem["s_%d" % rank])], 2 * w)
+    send_cross()
+    g.wait_ge(sem["bq%d" % BX], 1)
+    send(feed(BX, "f0", every))
+    g.wait_ge(sem["bq%d" % BY], 1)
+    send(feed(BY, "f1", every))
+    g.wait_ge(sem["bq%d" % BZ], 1)
+    send(feed(BZ, "n0a", hi), direct(BX))
+    g.wait_ge(sem["bq%d" % BW], 1)
+    send(feed(BW, "n1", hi[1::2]), feed(BW, "n0b", hi[0::2]),
+         (T.bs[:], [T.bins[:, 512 * rank:512 * rank + 512]] * 3, [cores[d] for d in (ca, cb, peer)], lo, sem["s_%d" % rank]))
+    send(direct(BY))
     g.wait_ge(sem.sent, nsent[0])
 
     V.memset(T.lf[0:32, :], 0.0).then_inc(sem.ms, 1)
@@ -198,31 +223,34 @@ def rank_program(g, core, T, topo):
         V.wait_ge(sem["sg%d" % t], 16)
         V.tensor_copy(T.bb[:, t:2048:4], T.w2g[:, 512 * t:512 * t + 512]).then_inc(sem.bc4, 1)
 
+    def quantise_b():
+        for t in range(1, 3):
+            spread(t)
+        V.wait_ge(sem.sg3, 16)
+        S.wait_ge(sem.sg3, 16)
+        for o in (BX, BY, BZ, BW):
+            dst, src = T.bb[:, 512 * o + 3:512 * o + 512:4], T.w2g[:, 1536 + 128 * o:1536 + 128 * o + 128]
+            if o == BX:
+                V.tensor_copy(dst, src).then_inc(sem.bc4, 1)
+                V.wait_ge(sem.bc4, 4)
+            else:
+                S.activation(dst, src, ActivationFunctionType.Copy).then_inc(sem["bc%d" % o], 1)
+                V.wait_ge(sem["bc%d" % o], 1)
+            V.quantize_mx(T.bq[:, 128 * o:128 * o + 128], T.bs[:, 128 * o:128 * o + 128],
+                          T.bb[:, 512 * o:512 * o + 512]).then_inc(sem["bq%d" % o], 1)
+
     TE.wait_ge(sem.xqd, 1)
     TE.wait_ge(sem.aqd, 1)
-    arrival = [2] + sorted(range(2), key=lambda k: slots(sl[k], cores, topo).index(rank)) + [3]
     spread(0)
-    for i, k in enumerate(arrival):
+    for i, k in enumerate(arr):
         ps = T.yp if i % 2 else T.zp
         cols = slice(T_ * k, T_ * k + T_)
         if sl[k] != rank:
             TE.wait_ge(sem["x_%d" % sl[k]], 2 * len(ex))
         else:
-            for t in range(1, 3):
-                spread(t)
-            V.wait_ge(sem.sg3, 16)
-            V.tensor_copy(T.bb[:, 1536 + 3:2048:4], T.w2g[:, 1536 + 384:2048]).then_inc(sem.bc4, 1)
-            S.wait_ge(sem.sg3, 16)
-            S.activation(T.bb[:, 512 + 3:1536:4], T.w2g[:, 1536 + 128:1536 + 384], ActivationFunctionType.Copy).then_inc(sem.bc1, 1)
-            S.activation(T.bb[:, 3:512:4], T.w2g[:, 1536:1536 + 128], ActivationFunctionType.Copy).then_inc(sem.bc2, 1)
-            V.wait_ge(sem.bc4, 4)
-            V.quantize_mx(T.bq[:, 384:512], T.bs[:, 384:512], T.bb[:, 1536:2048]).then_inc(sem.bq0, 1)
-            V.wait_ge(sem.bc1, 1)
-            V.quantize_mx(T.bq[:, 128:384], T.bs[:, 128:384], T.bb[:, 512:1536]).then_inc(sem.bq1, 1)
-            V.wait_ge(sem.bc2, 1)
-            V.quantize_mx(T.bq[:, 0:128], T.bs[:, 0:128], T.bb[:, 0:512]).then_inc(sem.bq2, 1)
+            quantise_b()
         if i >= 2:
-            TE.wait_ge(sem["hr%d" % arrival[i - 2]], 4)
+            TE.wait_ge(sem["hr%d" % arr[i - 2]], 4)
         for b in range(4):
             TE.matmul_mx(ps[:, 512 * b:512 * b + T_], T.aq[:, 128 * b:128 * b + 128], T.as_[:, 128 * b:128 * b + 128],
                          T.xq[:, cols], T.xs[:, cols], True, True).then_inc(sem["z%d_%d" % (k, b)], 1)
@@ -236,20 +264,22 @@ def rank_program(g, core, T, topo):
         V.wait_ge(sem["hr%d" % k], 4)
         V.quantize_mx(T.hq[:, cols], T.hs[:, cols], T.hb[:, 4 * T_ * k:4 * T_ * k + 4 * T_]).then_inc(sem["hq%d" % k], 1)
 
-    for j in range(3):
-        TE.wait_ge(sem["bq%d" % j], 1)
+    for o in range(4):
+        TE.wait_ge(sem["bq%d" % o], 1)
     TE.wait_ge(sem.hq3, 1)
-    TE.wait_ge(sem["hr%d" % arrival[3]], 4)
+    TE.wait_ge(sem["hr%d" % arr[3]], 4)
     for o in range(4):
         TE.matmul_mx(T.yp[:, 512 * o:512 * o + 128], T.bq[:, 128 * o:128 * o + 128], T.bs[:, 128 * o:128 * o + 128],
                      T.hq[:, own], T.hs[:, own], True, False)
-    parts = sorted([(order(s, o, cores, topo).index(rank), o, s) for s in others for o in range(4)])
-    seen, left = [], [3] * 4
-    for _, o, s in parts:
+    sa = [s for s in cross if dests(s, cores, topo)[1] == rank][0]
+    sb = [s for s in cross if s != sa][0]
+    parts = [(sa, BZ), (sb, BZ), (peer, BX), (sb, BW), (sa, BW), (peer, BZ), (sa, BX), (peer, BW), (sb, BY), (sb, BX), (sa, BY), (peer, BY)]
+    seen, left, done = [], [3] * 4, []
+    for s, o in parts:
         if s not in seen:
             seen.append(s)
             TE.wait_ge(sem["s_%d" % s], w)
-            TE.wait_ge(sem["h_%d" % s], w // 2 + (4 * w if s == peer else w))
+            TE.wait_ge(sem["h_%d" % s], 5 * w if s == peer else 2 * w)
         TE.wait_ge(sem["c_%d_%d" % (s, o)], w)
         left[o] -= 1
         a = 512 * s + 128 * o
@@ -257,42 +287,78 @@ def rank_program(g, core, T, topo):
                          T.hinq[:, T_ * s:T_ * s + T_], T.hins[:, T_ * s:T_ * s + T_], False, left[o] == 0)
         if left[o] == 0:
             m.then_inc(sem["yo%d" % o], 1)
+            done.append(o)
 
-    for half in range(2):
-        o = 2 * half
-        V.wait_ge(sem["yo%d" % o], 1)
-        V.tensor_copy(T.ysb[:, T_ * o:T_ * o + T_], T.yp[:, 512 * o:512 * o + 128]).then_inc(sem["yc%d" % o], 1)
-        SY.wait_ge(sem["yc%d" % o], 1)
-        SY.dma_start(T.y[:, T_ * o:T_ * o + T_], T.ysb[:, T_ * o:T_ * o + T_]).then_inc(sem.st0, 16)
-        o = 2 * half + 1
-        S.wait_ge(sem["yo%d" % o], 1)
-        S.activation(T.ysb[:, T_ * o:T_ * o + T_], T.yp[:, 512 * o:512 * o + 128], ActivationFunctionType.Copy).then_inc(sem["yc%d" % o], 1)
-        S.wait_ge(sem["yc%d" % o], 1)
-        S.dma_start(T.y[:, T_ * o:T_ * o + T_], T.ysb[:, T_ * o:T_ * o + T_]).then_inc(sem.st1, 16)
+    for i, o in enumerate(done):
+        dst, src = T.ysb[:, T_ * o:T_ * o + T_], T.yp[:, 512 * o:512 * o + 128]
+        if i % 2 == 0:
+            V.wait_ge(sem["yo%d" % o], 1)
+            V.tensor_copy(dst, src).then_inc(sem["yc%d" % (i // 2)], 1)
+        else:
+            S.wait_ge(sem["yo%d" % o], 1)
+            S.activation(dst, src, ActivationFunctionType.Copy).then_inc(sem["yc%d" % (i // 2)], 1)
+            a = T_ * min(o, done[i - 1])
+            SY.wait_ge(sem["yc%d" % (i // 2)], 2)
+            SY.dma_start(T.y[:, a:a + 2 * T_], T.ysb[:, a:a + 2 * T_]).then_inc(sem.st0, 16)
     SY.wait_ge(sem.st0, 32)
-    S.wait_ge(sem.st1, 32)
 
 
-def hand_on(g, core, s, o, T, topo, copy):
+def hand_on(g, core, s, role, T, topo, copy):
     sem = T.sem
+    u8 = dt.uint8
     cores = list(T.cores)
-    peer = slots(s, cores, topo)[2]
-    lo = topo.engines(core, cores[peer])
-    fh, fb = feeds(s, cores, topo)
-    a = T_ * s + XP * o
-    g.wait_ge(sem.rx, len(fh[o]))
-    g.remote_dma_fused([copy(T.rlx[:].bitcast(dt.uint8), [T.hinq[:, a:a + XP].bitcast(dt.uint8)], [cores[peer]], lo, sem["h_%d" % s])],
-                       local_sem=sem.sent)
-    calls = 2
-    if o in (1, 2):
-        d = slots(s, cores, topo)[o - 1]
-        g.wait_ge(sem.rh, len(fb[o]))
-        g.remote_dma_fused([copy(T.rlh[:].bitcast(dt.uint8), [T.hinq[:, T_ * s:T_ * s + T_].bitcast(dt.uint8)], [cores[d]], lo, sem["h_%d" % s])],
-                           local_sem=sem.sent)
-        calls = 3
-    to = [cores[d] for d in order(s, o, cores, topo)]
-    a = 512 * s + 128 * o
-    g.wait_ge(sem.rc, len(fb[o]))
-    g.remote_dma_fused([copy(T.rlq[:].bitcast(dt.uint8), [T.binq[:, a:a + 128].bitcast(dt.uint8)] * len(to), to, lo, sem["c_%d_%d" % (s, o)])],
-                       local_sem=sem.sent)
-    g.wait_ge(sem.sent, calls * len(lo))
+    peer, ca, cb = dests(s, cores, topo)
+    lo, hi = engines(s, cores, topo)
+    w = len(lo)
+    calls = [0]
+
+    def send(src, dsts, to, rsem):
+        g.remote_dma_fused([copy(src, dsts, to, lo, rsem)], local_sem=sem.sent)
+        calls[0] += 1
+
+    def slot(q):
+        return T.rlq[:, 128 * q:128 * q + 128].bitcast(u8)
+
+    def deliver(q, o, ds):
+        a = 512 * q + 128 * o
+        send(slot(q), [T.binq[:, a:a + 128].bitcast(u8)] * len(ds), [cores[d] for d in ds], sem["c_%d_%d" % (q, o)])
+
+    def plane_h(q, d, half):
+        send(T.rlp[:, T_ * half:T_ * half + T_], [T.hins[:, T_ * q:T_ * q + T_]], [cores[d]], sem["h_%d" % q])
+
+    def codes_h(q, d, half):
+        send(T.rlh[:, T_ * half:T_ * half + T_].bitcast(u8), [T.hinq[:, T_ * q:T_ * q + T_].bitcast(u8)], [cores[d]], sem["h_%d" % q])
+
+    def part_h(q, d):
+        a = T_ * q + XP * PARTS.index(role)
+        g.wait_ge(sem.rx, w // 2)
+        send(T.rlx[:].bitcast(u8), [T.hinq[:, a:a + XP].bitcast(u8)], [cores[d]], sem["h_%d" % q])
+
+    if role in ("m0", "m1"):
+        sa = [q for q in (ca, cb) if dests(q, cores, topo)[1] == s][0]
+        sb = [q for q in (ca, cb) if q != sa][0]
+        g.wait_ge(sem.rh0, w)
+        if role == "m0":
+            plane_h(sa, s, 1)
+        else:
+            codes_h(sa, s, 0)
+        for q in ((sa, sb) if role == "m0" else (sb, sa)):
+            g.wait_ge(sem["rc%d" % q], w)
+            deliver(q, BX if role == "m0" else BY, [s])
+    else:
+        if role in PARTS:
+            part_h(s, peer)
+        else:
+            g.wait_ge(sem.rx, 2 * w)
+            plane_h(s, peer, 0)
+        if role in ("n1", "n0b"):
+            g.wait_ge(sem.rh1, w)
+            (plane_h if role == "n1" else codes_h)(s, cb, 1)
+        g.wait_ge(sem["rc%d" % s], {"f0": 2 * w, "f1": 2 * w, "n0a": w, "n1": w // 2, "n0b": w // 2}[role])
+        if role in ("f0", "f1"):
+            ds = (ca, cb) if role == "f0" else (cb, ca)
+            send(slot(s), [slot(s)] * 2, [helpers(d, cores, topo)["m" + role[1]] for d in ds], sem["rc%d" % s])
+        else:
+            o, ds = {"n0a": (BZ, [ca, cb, peer]), "n1": (BW, [ca, peer]), "n0b": (BW, [cb])}[role]
+            deliver(s, o, ds)
+    g.wait_ge(sem.sent, calls[0] * w)

from concourse.bass import DstId, RemoteDMATransfer, IndirectOffsetOnAxis
from concourse.mybir import dt, AluOpType, ActivationFunctionType

T_ = 128
HU = 1536
ACT = 512
NCORES = 112
F8 = "float8_e4m3fn_x4"
XP = T_ // 4
X_AFTER = 0

SCRATCH = {
    "actb": ("sbuf", [128, 4], "int32"),
    "lst": ("sbuf", [128, 64], "int32"),
    "lf": ("sbuf", [128, 128], "float32"),
    "lt": ("sbuf", [128, 128], "float32"),
    "lc": ("sbuf", [128, 32], "float32"),
    "off": ("sbuf", [128, 128], "uint16"),
    "xb": ("sbuf", [128, 4 * T_], "bfloat16"),
    "w1b": ("sbuf", [128, 4 * HU], "bfloat16"),
    "ab": ("sbuf", [128, 4 * ACT], "bfloat16"),
    "w2g": ("sbuf", [128, 4 * 512], "bfloat16"),
    "bb": ("sbuf", [128, 4 * 512], "bfloat16"),
    "hb": ("sbuf", [128, 4 * 4 * T_], "bfloat16"),
    "xq": ("sbuf", [128, 4 * T_], F8), "xs": ("sbuf", [128, 4 * T_], "uint8"),
    "aq": ("sbuf", [128, ACT], F8), "as_": ("sbuf", [128, ACT], "uint8"),
    "bq": ("sbuf", [128, 512], F8), "bs": ("sbuf", [128, 512], "uint8"),
    "hq": ("sbuf", [128, 4 * T_], F8), "hs": ("sbuf", [128, 4 * T_], "uint8"),
    "hinq": ("sbuf", [128, 4 * T_], F8), "hins": ("sbuf", [128, 4 * T_], "uint8"),
    "binq": ("sbuf", [128, 4 * 512], F8), "bins": ("sbuf", [128, 4 * 512], "uint8"),
    "rlx": ("sbuf", [128, XP], F8), "rlh": ("sbuf", [128, 2 * T_], F8),
    "rlp": ("sbuf", [128, 2 * T_], "uint8"), "rlq": ("sbuf", [128, 4 * 128], F8),
    "ysb": ("sbuf", [128, 4 * T_], "float32"),
    "zp": ("psum", [128, 2048], "float32"),
    "yp": ("psum", [128, 2048], "float32"),
}
SEMAPHORES = (["d_act", "d_x", "d_lst", "d_w1", "ms", "xqd", "lf8", "tr", "lc4", "of4", "ofa", "ag4", "aqd", "bc4",
               "rx", "rh0", "rh1", "sent", "st0", "st1"]
              + ["bc%d" % o for o in range(4)] + ["bq%d" % o for o in range(4)] + ["rc%d" % s for s in range(4)]
              + ["sg%d" % t for t in range(4)] + ["z%d_%d" % (k, b) for k in range(4) for b in range(4)]
              + ["hr%d" % k for k in range(4)] + ["hq%d" % k for k in range(4)]
              + ["yo%d" % o for o in range(4)] + ["yc%d" % o for o in range(4)]
              + ["x_%d" % s for s in range(4)] + ["h_%d" % s for s in range(4)] + ["s_%d" % s for s in range(4)]
              + ["c_%d_%d" % (s, o) for s in range(4) for o in range(4)])
BX, BY, BZ, BW = 3, 2, 1, 0


def bits(es):
    m = 0
    for e in es:
        m |= 1 << e
    return m


def slots(r, cores, topo):
    rest = [(r + k) % len(cores) for k in range(1, len(cores))]
    peer = [s for s in rest if topo.same_plane(topo.chip(cores[r]), topo.chip(cores[s]))]
    return [s for s in rest if s not in peer] + peer + [r]


def arrival(r, cores, topo):
    sl = slots(r, cores, topo)
    return [2] + sorted(range(2), key=lambda k: slots(sl[k], cores, topo).index(r)) + [3]


def dests(s, cores, topo):
    sl = slots(s, cores, topo)
    return [sl[k] for k in arrival(s, cores, topo)[0:3]]


def helpers(s, cores, topo):
    me = cores[s]
    near = [c for c in topo.cores_of(me) if c != me]
    able = [c for c in near if all(topo.may_write(c, d) for d in cores)]
    rest = [c for c in near if c not in able]
    mate = [c for c in range(NCORES) if topo.mates(topo.chip(c), topo.chip(me)) and topo.may_write(c, me)]

    def on(cs, same):
        return [c for c in cs if (topo.die(c) == topo.die(me)) == same]

    return {"n1": on(able, True)[0], "n0a": on(able, False)[0], "n0b": on(able, False)[1],
            "f1": on(rest, True)[0], "f0": on(rest, False)[0], "m1": on(mate, True)[0], "m0": on(mate, False)[0]}


def engines(s, cores, topo):
    lo = topo.engines(cores[s], cores[(s + 1) % len(cores)])
    return lo, [e for e in topo.engines(cores[s], helpers(s, cores, topo)["n1"]) if e not in lo]


PARTS = ["f0", "n0b", "f1", "n0a"]


def rank_program(g, core, T, topo):
    rank = T.rank_of(core)
    cores = list(T.cores)
    n = len(cores)
    sem = T.sem
    u8 = dt.uint8

    def copy(src, dsts, to, engines, rsem):
        ids = [DstId(rid=topo.addr(c)[0], pnc=topo.addr(c)[1]) for c in to]
        return RemoteDMATransfer(dst_ids=ids, dma_engine_mask=bits(engines), remote_sem=rsem, srcs=[src], dsts=dsts)

    def place(d, s):
        return T_ * slots(d, cores, topo).index(s)

    if rank is None:
        for s in range(n):
            for role, c in helpers(s, cores, topo).items():
                if c == core:
                    hand_on(g, core, s, role, T, topo, copy)
        return

    sl = slots(rank, cores, topo)
    arr = arrival(rank, cores, topo)
    cross = sl[0:2]
    peer, ca, cb = dests(rank, cores, topo)
    hp = helpers(rank, cores, topo)
    lo, hi = engines(rank, cores, topo)
    every = lo + hi
    own = slice(3 * T_, 4 * T_)
    w = len(lo)
    ex = lo

    V, S, TE, SY = g.vector, g.scalar, g.tensor, g.sync

    SY.dma_start(T.actb[:], T.act[:]).then_inc(sem.d_act, 16)
    S.dma_start(T.lst[0:8, :], T.act[:]).then_inc(sem.d_lst, 16)
    SY.dma_start(T.xb[:], T.x[:]).then_inc(sem.d_x, 16)
    SY.dma_start(T.w1b[:], T.w1[:]).then_inc(sem.d_w1, 16)

    nsent = [0]

    def send(*moves):
        g.remote_dma_fused([copy(*m) for m in moves], local_sem=sem.sent)
        nsent[0] += sum(len(m[3]) for m in moves)

    def send_x():
        g.wait_ge(sem.xqd, 1)
        ds = [peer] + cross
        to = [cores[d] for d in ds]
        send((T.xs[:, own], [T.xs[:, place(d, rank):place(d, rank) + T_] for d in ds], to, ex, sem["x_%d" % rank]))
        send((T.xq[:, own].bitcast(u8), [T.xq[:, place(d, rank):place(d, rank) + T_].bitcast(u8) for d in ds], to, ex, sem["x_%d" % rank]))

    def send_h():
        g.wait_ge(sem.hq2, 1)
        for pair in ((0, 1), (2, 3)):
            send(*[(T.hq[:, 2 * T_ + XP * i:2 * T_ + XP * i + XP].bitcast(u8), [T.rlx[:].bitcast(u8)], [hp[PARTS[i]]],
                    every[4 * i:4 * i + 4], sem.rx) for i in pair])
        send((T.hs[:, 2 * T_:3 * T_], [T.rlp[:, 0:T_]], [hp["n1"]], every, sem.rx))

    def send_cross():
        far = helpers(ca, cores, topo)
        for i, (k, rp, rq, e) in enumerate(((arr[1], far["m0"], far["m1"], lo), (arr[2], hp["n1"], hp["n0b"], hi))):
            g.wait_ge(sem["hq%d" % k], 1)
            send((T.hs[:, T_ * k:T_ * k + T_], [T.rlp[:, T_:2 * T_]], [rp], e, sem["rh%d" % i]))
            send((T.hq[:, T_ * k:T_ * k + T_].bitcast(u8), [T.rlh[:, T_ * i:T_ * i + T_].bitcast(u8)], [rq], e, sem["rh%d" % i]))

    def block(o):
        return T.bq[:, 128 * o:128 * o + 128].bitcast(u8)

    def feed(o, role, e):
        return block(o), [T.rlq[:, 128 * rank:128 * rank + 128].bitcast(u8)], [hp[role]], e, sem["rc%d" % rank]

    def direct(o):
        a = 512 * rank + 128 * o
        return block(o), [T.binq[:, a:a + 128].bitcast(u8)], [cores[peer]], lo, sem["c_%d_%d" % (rank, o)]

    g.wait_ge(sem.d_act, 16)
    for t in range(4):
        g.indirect_dma_start(T.w2g[:, 512 * t:512 * t + 512], None, T.w2[:],
                             IndirectOffsetOnAxis(ap=T.actb[:, t:t + 1], axis=0),
                             bounds_check=HU - 1).then_inc(sem["sg%d" % t], 16)
        if t == X_AFTER:
            send_x()
    send_h()
    send_cross()
    g.wait_ge(sem["bq%d" % BX], 1)
    send(feed(BX, "f0", every))
    g.wait_ge(sem["bq%d" % BY], 1)
    send(feed(BY, "f1", every))
    g.wait_ge(sem["bq%d" % BZ], 1)
    send(feed(BZ, "n0a", hi), direct(BX))
    g.wait_ge(sem["bq%d" % BW], 1)
    send(feed(BW, "n1", hi[1::2]), feed(BW, "n0b", hi[0::2]),
         (T.bs[:], [T.bins[:, 512 * rank:512 * rank + 512]] * 3, [cores[d] for d in (ca, cb, peer)], lo, sem["s_%d" % rank]))
    send(direct(BY))
    g.wait_ge(sem.sent, nsent[0])

    V.memset(T.lf[0:32, :], 0.0).then_inc(sem.ms, 1)
    V.wait_ge(sem.ms, 1)
    V.wait_ge(sem.d_lst, 16)
    for b in range(4):
        for h in range(2):
            V.tensor_scalar(T.lf[0:8, 32 * b + 16 * h:32 * b + 16 * h + 16], T.lst[0:8, b:64:4], 4.0, None, AluOpType.mult).then_inc(sem.lf8, 1)
    V.wait_ge(sem.d_x, 16)
    V.quantize_mx(T.xq[:, own], T.xs[:, own], T.xb[:]).then_inc(sem.xqd, 1)
    V.wait_ge(sem.lf8, 8)
    V.transpose(T.lt[0:32, :], T.lf[0:32, :]).then_inc(sem.tr, 1)
    V.wait_ge(sem.tr, 1)
    for b in range(4):
        V.tensor_copy(T.lc[0:32, 8 * b:8 * b + 8], T.lt[0:32, 32 * b:32 * b + 8]).then_inc(sem.lc4, 1)
    V.wait_ge(sem.lc4, 4)
    for t in range(4):
        V.tensor_scalar(T.off[0:32, 32 * t:32 * t + 32], T.lc[0:32, :], float(t), None, AluOpType.add).then_inc(sem.of4, 1)
    V.wait_ge(sem.of4, 4)
    for q in range(1, 4):
        V.tensor_copy(T.off[32 * q:32 * q + 32, :], T.off[0:32, :]).then_inc(sem.ofa, 1)
    V.wait_ge(sem.ofa, 3)
    S.wait_ge(sem.ofa, 3)
    V.wait_ge(sem.d_w1, 16)
    S.wait_ge(sem.d_w1, 16)
    for t in range(4):
        win = T.w1b[:, 0:4 * HU].indirect(T.off[:, 32 * t:32 * t + 32])
        if t < 2:
            S.activation(T.ab[:, t:2048:4], win, ActivationFunctionType.Copy).then_inc(sem.ag4, 1)
        else:
            V.tensor_copy(T.ab[:, t:2048:4], win).then_inc(sem.ag4, 1)
    V.wait_ge(sem.ag4, 4)
    V.quantize_mx(T.aq[:], T.as_[:], T.ab[:]).then_inc(sem.aqd, 1)

    def spread(t):
        V.wait_ge(sem["sg%d" % t], 16)
        V.tensor_copy(T.bb[:, t:2048:4], T.w2g[:, 512 * t:512 * t + 512]).then_inc(sem.bc4, 1)

    def quantise_b():
        for t in range(1, 3):
            spread(t)
        V.wait_ge(sem.sg3, 16)
        S.wait_ge(sem.sg3, 16)
        for o in (BX, BY, BZ, BW):
            dst, src = T.bb[:, 512 * o + 3:512 * o + 512:4], T.w2g[:, 1536 + 128 * o:1536 + 128 * o + 128]
            if o == BX:
                V.tensor_copy(dst, src).then_inc(sem.bc4, 1)
                V.wait_ge(sem.bc4, 4)
            else:
                S.activation(dst, src, ActivationFunctionType.Copy).then_inc(sem["bc%d" % o], 1)
                V.wait_ge(sem["bc%d" % o], 1)
            V.quantize_mx(T.bq[:, 128 * o:128 * o + 128], T.bs[:, 128 * o:128 * o + 128],
                          T.bb[:, 512 * o:512 * o + 512]).then_inc(sem["bq%d" % o], 1)

    TE.wait_ge(sem.xqd, 1)
    TE.wait_ge(sem.aqd, 1)
    spread(0)
    for i, k in enumerate(arr):
        ps = T.yp if i % 2 else T.zp
        cols = slice(T_ * k, T_ * k + T_)
        if sl[k] != rank:
            TE.wait_ge(sem["x_%d" % sl[k]], 2 * len(ex))
        else:
            quantise_b()
        if i >= 2:
            TE.wait_ge(sem["hr%d" % arr[i - 2]], 4)
        for b in range(4):
            TE.matmul_mx(ps[:, 512 * b:512 * b + T_], T.aq[:, 128 * b:128 * b + 128], T.as_[:, 128 * b:128 * b + 128],
                         T.xq[:, cols], T.xs[:, cols], True, True).then_inc(sem["z%d_%d" % (k, b)], 1)
            dst, src = T.hb[:, 4 * T_ * k + b:4 * T_ * k + 4 * T_:4], ps[:, 512 * b:512 * b + T_]
            if b % 2:
                V.wait_ge(sem["z%d_%d" % (k, b)], 1)
                V.tensor_scalar(dst, src, 0.05, 0.0, AluOpType.mult, AluOpType.max).then_inc(sem["hr%d" % k], 1)
            else:
                S.wait_ge(sem["z%d_%d" % (k, b)], 1)
                S.activation(dst, src, ActivationFunctionType.Relu, scale=0.05).then_inc(sem["hr%d" % k], 1)
        V.wait_ge(sem["hr%d" % k], 4)
        V.quantize_mx(T.hq[:, cols], T.hs[:, cols], T.hb[:, 4 * T_ * k:4 * T_ * k + 4 * T_]).then_inc(sem["hq%d" % k], 1)

    for o in range(4):
        TE.wait_ge(sem["bq%d" % o], 1)
    TE.wait_ge(sem.hq3, 1)
    TE.wait_ge(sem["hr%d" % arr[3]], 4)
    for o in range(4):
        TE.matmul_mx(T.yp[:, 512 * o:512 * o + 128], T.bq[:, 128 * o:128 * o + 128], T.bs[:, 128 * o:128 * o + 128],
                     T.hq[:, own], T.hs[:, own], True, False)
    sa = [s for s in cross if dests(s, cores, topo)[1] == rank][0]
    sb = [s for s in cross if s != sa][0]
    parts = [(sa, BZ), (sb, BZ), (peer, BX), (sb, BW), (sa, BW), (peer, BZ), (sa, BX), (peer, BW), (sb, BY), (sb, BX), (sa, BY), (peer, BY)]
    seen, left, done = [], [3] * 4, []
    for s, o in parts:
        if s not in seen:
            seen.append(s)
            TE.wait_ge(sem["s_%d" % s], w)
            TE.wait_ge(sem["h_%d" % s], 5 * w if s == peer else 2 * w)
        TE.wait_ge(sem["c_%d_%d" % (s, o)], w)
        left[o] -= 1
        a = 512 * s + 128 * o
        m = TE.matmul_mx(T.yp[:, 512 * o:512 * o + 128], T.binq[:, a:a + 128], T.bins[:, a:a + 128],
                         T.hinq[:, T_ * s:T_ * s + T_], T.hins[:, T_ * s:T_ * s + T_], False, left[o] == 0)
        if left[o] == 0:
            m.then_inc(sem["yo%d" % o], 1)
            done.append(o)

    for i, o in enumerate(done):
        dst, src = T.ysb[:, T_ * o:T_ * o + T_], T.yp[:, 512 * o:512 * o + 128]
        if i % 2 == 0:
            V.wait_ge(sem["yo%d" % o], 1)
            V.tensor_copy(dst, src).then_inc(sem["yc%d" % (i // 2)], 1)
        else:
            S.wait_ge(sem["yo%d" % o], 1)
            S.activation(dst, src, ActivationFunctionType.Copy).then_inc(sem["yc%d" % (i // 2)], 1)
            a = T_ * min(o, done[i - 1])
            SY.wait_ge(sem["yc%d" % (i // 2)], 2)
            SY.dma_start(T.y[:, a:a + 2 * T_], T.ysb[:, a:a + 2 * T_]).then_inc(sem.st0, 16)
    SY.wait_ge(sem.st0, 32)


def hand_on(g, core, s, role, T, topo, copy):
    sem = T.sem
    u8 = dt.uint8
    cores = list(T.cores)
    peer, ca, cb = dests(s, cores, topo)
    lo, hi = engines(s, cores, topo)
    w = len(lo)
    calls = [0]

    def send(src, dsts, to, rsem):
        g.remote_dma_fused([copy(src, dsts, to, lo, rsem)], local_sem=sem.sent)
        calls[0] += 1

    def slot(q):
        return T.rlq[:, 128 * q:128 * q + 128].bitcast(u8)

    def deliver(q, o, ds):
        a = 512 * q + 128 * o
        send(slot(q), [T.binq[:, a:a + 128].bitcast(u8)] * len(ds), [cores[d] for d in ds], sem["c_%d_%d" % (q, o)])

    def plane_h(q, d, half):
        send(T.rlp[:, T_ * half:T_ * half + T_], [T.hins[:, T_ * q:T_ * q + T_]], [cores[d]], sem["h_%d" % q])

    def codes_h(q, d, half):
        send(T.rlh[:, T_ * half:T_ * half + T_].bitcast(u8), [T.hinq[:, T_ * q:T_ * q + T_].bitcast(u8)], [cores[d]], sem["h_%d" % q])

    def part_h(q, d):
        a = T_ * q + XP * PARTS.index(role)
        g.wait_ge(sem.rx, w // 2)
        send(T.rlx[:].bitcast(u8), [T.hinq[:, a:a + XP].bitcast(u8)], [cores[d]], sem["h_%d" % q])

    if role in ("m0", "m1"):
        sa = [q for q in (ca, cb) if dests(q, cores, topo)[1] == s][0]
        sb = [q for q in (ca, cb) if q != sa][0]
        g.wait_ge(sem.rh0, w)
        if role == "m0":
            plane_h(sa, s, 1)
        else:
            codes_h(sa, s, 0)
        for q in ((sa, sb) if role == "m0" else (sb, sa)):
            g.wait_ge(sem["rc%d" % q], w)
            deliver(q, BX if role == "m0" else BY, [s])
    else:
        if role in PARTS:
            part_h(s, peer)
        else:
            g.wait_ge(sem.rx, 2 * w)
            plane_h(s, peer, 0)
        if role in ("n1", "n0b"):
            g.wait_ge(sem.rh1, w)
            (plane_h if role == "n1" else codes_h)(s, cb, 1)
        g.wait_ge(sem["rc%d" % s], {"f0": 2 * w, "f1": 2 * w, "n0a": w, "n1": w // 2, "n0b": w // 2}[role])
        if role in ("f0", "f1"):
            ds = (ca, cb) if role == "f0" else (cb, ca)
            send(slot(s), [slot(s)] * 2, [helpers(d, cores, topo)["m" + role[1]] for d in ds], sem["rc%d" % s])
        else:
            o, ds = {"n0a": (BZ, [ca, cb, peer]), "n1": (BW, [ca, peer]), "n0b": (BW, [cb])}[role]
            deliver(s, o, ds)
    g.wait_ge(sem.sent, calls[0] * w)
